import numpy as np
import ml_dtypes


def mxq(x, axis, fmt="e4m3"):
    dtype, down = {"e4m3": (ml_dtypes.float8_e4m3fn, 7), "e5m2": (ml_dtypes.float8_e5m2, 14)}[fmt]
    v = np.moveaxis(np.asarray(x, np.float32).astype(ml_dtypes.bfloat16).astype(np.float64), axis, -1)
    blocks = v.reshape(v.shape[:-1] + (-1, 32))
    amax = np.abs(blocks).max(-1, keepdims=True)
    byte = np.maximum(np.where(amax > 0, np.frexp(amax)[1] - 1 + 127, 0) - down, 1)
    scale = np.exp2(byte - 127.0)
    codes = (blocks / scale).astype(np.float32).astype(dtype).astype(np.float64)
    return np.moveaxis((codes * scale).reshape(v.shape), -1, axis)


WIDE = False


def mx_kscale(k):
    if not WIDE:
        return np.ones(k)
    levels = np.array([10, -10, 5, -5, 0])
    if k % 512:
        return np.exp2(np.random.permutation(np.resize(levels, k // 32))).repeat(32)
    a = np.empty((k // 512, 16))
    for p in range(k // 512):
        a[p, :8] = np.random.permutation(np.resize(levels, 8))
        for g in range(8):
            far = levels[np.abs(levels - a[p, g]) >= 10]
            a[p, g + 8] = far[np.random.randint(len(far))]
    return np.exp2(a.ravel()).repeat(32)


BF16 = ml_dtypes.bfloat16


def bf(x):
    return np.asarray(x, np.float32).astype(BF16)


def f64(x):
    return np.asarray(x).astype(np.float64)


E2M1 = np.array([0.0, 0.5, 1.0, 1.5, 2.0, 3.0, 4.0, 6.0, -0.0, -0.5, -1.0, -1.5, -2.0, -3.0, -4.0, -6.0])


def pack_weight(w, fmt):
    k, n = w.shape
    w = f64(bf(w)).reshape(k // 32, 32, n)
    amax = np.abs(w).max(1)
    if fmt == "e4m3":
        byte = np.frexp(amax)[1] - 1 + 127 - 7
    else:
        mant, ex = np.frexp(amax / 6.0)
        byte = np.where(mant > 0.5, ex, ex - 1) + 127
    byte = np.clip(np.where(amax > 0, byte, 1), 1, 254)
    scaled = (w * np.exp2(127.0 - byte)[:, None, :]).reshape(k, n).astype(np.float32)
    by_word = np.ascontiguousarray(scaled.reshape(k // 512, 128, 4, n).transpose(0, 1, 3, 2))
    if fmt == "e4m3":
        words = by_word.astype(ml_dtypes.float8_e4m3fn).view(np.uint8)
    else:
        c = by_word.astype(ml_dtypes.float4_e2m1fn).view(np.uint8) & 0xF
        words = c[..., 0::2] | (c[..., 1::2] << 4)
    return np.ascontiguousarray(words), np.ascontiguousarray(byte.astype(np.uint8).reshape(k // 512, 16, n))


def unpack_weight(words, scales, fmt):
    g, p, n, _ = words.shape
    if fmt == "e4m3":
        vals = np.ascontiguousarray(words).view(ml_dtypes.float8_e4m3fn).astype(np.float64)
    else:
        nib = np.empty((g, p, n, 4), np.uint8)
        nib[..., 0::2] = words & 0xF
        nib[..., 1::2] = words >> 4
        vals = E2M1[nib]
    vals = vals * np.repeat(np.exp2(scales.astype(np.float64) - 127.0), 8, axis=1)[..., None]
    return vals.transpose(0, 1, 3, 2).reshape(g * 512, n)
def pack4(w):
    words, scales = pack_weight(w, "e2m1")
    return words.reshape(words.shape[0], 128, -1), scales


def unpack4(words, scales):
    return unpack_weight(words.reshape(words.shape[0], 128, -1, 2), scales, "e2m1")


M, K, N, R, L = 2048, 512, 1024, 1024, 1536


def draw0():
    s = mx_kscale(K)
    u = mx_kscale(L)
    t = mx_kscale(N)
    bits = np.random.beta(0.5, 0.5, (M, K))
    gen = np.random.standard_normal((K, N)) / np.sqrt(K)
    rx = np.random.standard_normal((R, L))
    filt = np.random.standard_normal((L, N)) / np.sqrt(L) / N ** 0.25
    amp = (1 + 0.3 * np.random.standard_normal(N)) / N ** 0.25
    gen_words, gen_scales = pack4(gen / s[:, None])
    return {"bits": bf(bits * s),
            "gen_words": gen_words,
            "gen_scales": gen_scales,
            "amp": bf(amp * t),
            "rx": bf(rx * u),
            "filt": bf(filt / u[:, None] / t)}


def core(bits, gen_words, gen_scales, amp, rx, filt):
    par = mxq(f64(bits), 1, "e4m3") @ unpack4(gen_words, gen_scales)
    code = np.cos(np.pi * par) * f64(amp)
    sym = mxq(f64(rx), 1, "e4m3") @ mxq(f64(filt), 0, "e4m3")
    return mxq(code, 1, "e4m3") @ mxq(sym, 1, "e4m3").T


def e4m3fn_bytes(y):
    return np.clip(np.asarray(y, np.float64), -448.0, 448.0).astype(np.float32).astype(ml_dtypes.float8_e4m3fn).view(np.uint8)


def e4m3fn_values(b):
    return np.asarray(b, np.uint8).view(ml_dtypes.float8_e4m3fn).astype(np.float64)


def setup_inputs():
    d = draw0()
    x0 = np.asarray(d['rx']).astype(np.float64)
    s = (np.max(np.abs(x0), axis=(0,), keepdims=True) / 448.0).astype(np.float32)
    out = {}
    for k, v in d.items():
        if k == 'rx':
            out['rx_bytes'] = e4m3fn_bytes(x0 / s.astype(np.float64))
            out['rx_scale'] = s
        else:
            out[k] = v
    return out


def reference(bits, gen_words, gen_scales, amp, rx_bytes, rx_scale, filt):
    return core(bits, gen_words, gen_scales, amp, e4m3fn_values(rx_bytes) * rx_scale.astype(np.float64), filt)

from contextlib import ExitStack

import concourse.mybir as mybir
from concourse.masks import make_identity

M, K, N, R, L = 2048, 512, 1024, 1024, 1536
FLOPS = 2 * (M * K * N + R * L * N + M * N * R)

F32 = mybir.dt.float32
BF16 = mybir.dt.bfloat16
I32 = mybir.dt.int32
U32 = mybir.dt.uint32
U8 = mybir.dt.uint8
F8 = mybir.dt.float8_e4m3fn
E4X4 = mybir.dt.float8_e4m3fn_x4
E2X4 = mybir.dt.float4_e2m1fn_x4
ALU = mybir.AluOpType
ACT = mybir.ActivationFunctionType

P = 128
TWO_PI = 6.283185307179586
GL = L // 512


def tile_parity_codebook_correlation_s11_kernel(tc, bits, gen_words, gen_scales, amp, rx_bytes, rx_scale, filt, out):
    nc = tc.nc
    with ExitStack() as ctx:
        keep = ctx.enter_context(tc.tile_pool(name="keep", bufs=1))
        work = ctx.enter_context(tc.tile_pool(name="work", bufs=2))
        psum = ctx.enter_context(tc.psum_pool(name="psum", bufs=1))

        g_sraw = keep.tile([P, N], U8, align_bytes=64)
        nc.vector.memset(g_sraw[:].bitcast(I32), 0)
        a_rows = keep.tile([P, P], BF16, align_bytes=64)
        nc.vector.memset(a_rows[:], 0.0)
        ident = keep.tile([P, P], F32, align_bytes=64)
        make_identity(nc, ident[:])
        ident_b = keep.tile([P, 8], BF16, align_bytes=64)
        nc.vector.tensor_copy(out=ident_b[:], in_=ident[:, 0:8])
        warm = keep.tile([P, 1], F32, align_bytes=64)
        nc.vector.memset(warm[:], 0.0)
        nc.scalar.activation(out=warm[:], in_=warm[:], func=ACT.Sin)

        bits_q = bits.rearrange("(q a p) k -> q p a k", a=2, p=P)
        rx_v = rx_bytes.rearrange("(s a p) l -> s p a l", a=2, p=P)
        filt_v = filt.rearrange("(g p j) n -> g p j n", p=P, j=4)
        g_wraw = keep.tile([P, 2 * N], U8, align_bytes=64)
        rx_sc = keep.tile([P, GL, 4], F32, align_bytes=64)
        bits_sb, rx_sb, filt_sb = {}, {}, {}

        def load(what):
            kind, i = what[0], int(what[1:] or 0)
            if kind == "b":
                b_raw = work.tile([P, 2, K], BF16, align_bytes=64, bufs=8)
                nc.sync.dma_start(out=b_raw[:], in_=bits_q[i])
                bits_sb[i] = b_raw
            elif kind == "x":
                rx_raw = work.tile([P, 2, L], U8, align_bytes=64, bufs=4)
                nc.sync.dma_start(out=rx_raw[:], in_=rx_v[i])
                rx_sb[i] = rx_raw
            elif kind == "f":
                f_raw = work.tile([P, 4, N], BF16, align_bytes=64, bufs=2)
                nc.sync.dma_start(out=f_raw[:], in_=filt_v[i])
                filt_sb[i] = f_raw
            elif kind == "g":
                nc.sync.dma_start(out=g_wraw[:].bitcast(I32), in_=gen_words[0].bitcast(I32))
                for quad in range(4):
                    nc.sync.dma_start(
                        out=g_sraw[32 * quad : 32 * quad + 4, :].bitcast(I32),
                        in_=gen_scales[0, 4 * quad : 4 * quad + 4, :].bitcast(I32),
                    )
            elif kind == "c":
                nc.sync.dma_start(out=rx_sc[:], in_=rx_scale.rearrange("o (g p t) -> p (o g) t", p=P, t=4))
            else:
                amp_v = amp.rearrange("(g q t i) -> g t q i", g=2, t=4, i=4)
                for g in range(2):
                    nc.sync.dma_start(out=a_rows[4 * g : 4 * g + 4, :].rearrange("t (q i) -> t q i", i=4), in_=amp_v[g])

        for what in ["b0","g","x0","f0","b1","x1","c","a","f1","x2","b2","f2","x3","b3","b4","b5","b6","b7"]:
            load(what)

        g_w = keep.tile([P, 2 * N], U8, align_bytes=64)
        g_s = keep.tile([P, N], U8, align_bytes=64)

        def permute_g():
            for g in range(2):
                w = slice(1024 * g, 1024 * g + 1024)
                nc.vector.tensor_copy(
                    out=g_w[:, w].bitcast(I32).rearrange("p (t q c) -> p t q c", t=4, c=2),
                    in_=g_wraw[:, w].bitcast(I32).rearrange("p (q t c) -> p t q c", t=4, c=2),
                )
                s = slice(512 * g, 512 * g + 512)
                nc.vector.tensor_copy(
                    out=g_s[:, s].bitcast(I32).rearrange("p (t q) -> p t q", t=4),
                    in_=g_sraw[:, s].bitcast(I32).rearrange("p (q t) -> p t q", t=4),
                )

        amp_sb = keep.tile([P, 8], F32, align_bytes=64)

        def turn_amp():
            pa = psum.tile([P, 8], F32, bufs=2, tag="turn", name="pa")
            nc.tensor.matmul(pa[:], lhsT=a_rows[:], rhs=ident_b[:], start=True, stop=True)
            nc.scalar.copy(out=amp_sb[:], in_=pa[:])

        box = {}

        b_codes = keep.tile([P, M], U32, align_bytes=64)
        b_scales = keep.tile([P, M], U8, align_bytes=64)

        def bits_halve(q):
            raw = bits_sb[q]
            nc.vector.tensor_scalar(out=raw[:], in0=raw[:], scalar1=0.5, scalar2=None, op0=ALU.mult)

        def bits_turn(q):
            words = bits_sb[q][:].rearrange("p a k -> p (a k)").bitcast(F32)
            pt = psum.tile([P, 2, 256], F32, bufs=2, tag="turn", name="pt")
            for a in range(2):
                for u in range(2):
                    nc.tensor.transpose(pt[:, u, 128 * a : 128 * a + 128], words[:, 256 * a + u : 256 * a + 256 : 2], ident[:])
            box["bT", q] = pt

        def bits_empty(q):
            grp = work.tile([P, 256, 4], BF16, align_bytes=64, name="b_grp", tag="b_grp")
            nc.scalar.activation(
                out=grp[:].rearrange("p r (u e) -> p r u e", e=2),
                in_=box["bT", q][:].rearrange("p u r -> p (u r)").bitcast(BF16).rearrange("p (u r e) -> p r u e", u=2, e=2),
                func=ACT.Copy, scale=0.5,
            )
            box["bE", q] = grp

        def bits_quant(q):
            nc.vector.quantize_mx(
                out=b_codes[:, 256 * q : 256 * q + 256].bitcast(E4X4),
                scales=b_scales[:, 256 * q : 256 * q + 256],
                in_=box["bE", q][:].rearrange("p r t -> p (r t)"),
            )

        x_codes = keep.tile([P, GL, R], U32, align_bytes=64)
        x_scales = keep.tile([P, GL, R], U8, align_bytes=64)

        def rx_widen(s, a):
            if a == 0:
                wide = work.tile([P, 2, L], BF16, align_bytes=64, name="wide", tag="wide")
                box["W", s] = wide
            engine = nc.vector if s == 0 else nc.gpsimd
            engine.tensor_copy(out=box["W", s][:, a, :], in_=rx_sb[s][:, a, :].bitcast(F8))

        def rx_turn(s, g):
            words = box["W", s][:].rearrange("p a l -> p (a l)").bitcast(F32)
            pt = psum.tile([P, 2, 256], F32, bufs=2, tag="turn", name="pt")
            for a in range(2):
                base = 768 * a + 256 * g
                for u in range(2):
                    nc.tensor.transpose(pt[:, u, 128 * a : 128 * a + 128], words[:, base + u : base + 256 : 2], ident[:])
            box["xT", s, g] = pt

        def rx_mult(s, g):
            grp = work.tile([P, 256, 4], BF16, align_bytes=64, bufs=3, name="x_grp", tag="x_grp")
            nc.vector.tensor_tensor(
                out=grp[:].rearrange("p r (u e) -> p r u e", e=2),
                in0=box["xT", s, g][:].rearrange("p u r -> p (u r)").bitcast(BF16).rearrange("p (u r e) -> p r u e", u=2, e=2),
                in1=rx_sc[:, g, :].rearrange("p (u e) -> p u e", e=2).unsqueeze(1).to_broadcast([P, 256, 2, 2]),
                op=ALU.mult,
            )
            box["xM", s, g] = grp

        def rx_quant(s, g):
            nc.vector.quantize_mx(
                out=x_codes[:, g, 256 * s : 256 * s + 256].bitcast(E4X4),
                scales=x_scales[:, g, 256 * s : 256 * s + 256],
                in_=box["xM", s, g][:].rearrange("p r t -> p (r t)"),
            )

        f_codes = keep.tile([P, GL, N], U32, align_bytes=64)
        f_scales = keep.tile([P, GL, N], U8, align_bytes=64)

        def filt_turn(g, h):
            grp = work.tile([P, 4, 32, 4, 4], BF16, align_bytes=64, bufs=2, name="f_grp", tag="f_grp")
            src = filt_sb[g][:, :, 512 * h : 512 * h + 512].rearrange("p j (q t i) -> p t q j i", t=4, i=4)
            dst = grp[:].rearrange("p t q i j -> p t q j i")
            for t in range(4):
                engine = "V" if 2 * g + h < 1 else "S"
                if engine == "S":
                    nc.scalar.copy(out=dst[:, t], in_=src[:, t])
                elif engine == "V":
                    nc.vector.tensor_copy(out=dst[:, t], in_=src[:, t])
                else:
                    nc.gpsimd.tensor_scalar(out=dst[:, t], in0=src[:, t], scalar1=1.0, scalar2=0.0, op0=ALU.mult, op1=ALU.add)
            box["F", g, h] = grp

        def filt_quant(g, h):
            nc.vector.quantize_mx(
                out=f_codes[:, g, 512 * h : 512 * h + 512].bitcast(E4X4),
                scales=f_scales[:, g, 512 * h : 512 * h + 512],
                in_=box["F", g, h][:].rearrange("p t q i j -> p (t q i j)"),
            )

        y_grp = keep.tile([P, 2, R, 4], BF16, align_bytes=64)
        y_codes = keep.tile([P, 2, R], U32, align_bytes=64)
        y_scales = keep.tile([P, 2, R], U8, align_bytes=64)

        def sym(rc, h):
            ps = psum.tile([P, 4, P], F32, bufs=3, tag="acc", name="ps")
            r = slice(P * rc, P * rc + P)
            for t in range(4):
                n = slice(512 * h + 128 * t, 512 * h + 128 * t + 128)
                for g in range(GL):
                    nc.tensor.matmul_mx(
                        out=ps[:, t, :],
                        lhsT=f_codes[:, g, n].bitcast(E4X4), lhsT_scale=f_scales[:, g, n],
                        rhs=x_codes[:, g, r].bitcast(E4X4), rhs_scale=x_scales[:, g, r],
                        start=(g == 0), stop=(g == GL - 1),
                    )
            box["sy", rc, h] = ps

        def sym_empty(rc, h):
            r = slice(P * rc, P * rc + P)
            nc.scalar.copy(out=y_grp[:, h, r, :], in_=box["sy", rc, h][:].rearrange("p t r -> p r t"))

        def sym_quant(h, rh):
            r = slice(512 * rh, 512 * rh + 512)
            nc.vector.quantize_mx(
                out=y_codes[:, h, r].bitcast(E4X4), scales=y_scales[:, h, r],
                in_=y_grp[:, h, r, :].rearrange("p r t -> p (r t)"),
            )

        def par(c, g):
            pp = psum.tile([P, 4, P], F32, bufs=3, tag="par", name="pp")
            m = slice(P * c, P * c + P)
            for t in range(4):
                n = slice(512 * g + 128 * t, 512 * g + 128 * t + 128)
                nc.tensor.matmul_mx(
                    out=pp[:, t, :],
                    lhsT=g_w[:, 2 * n.start : 2 * n.stop].bitcast(E2X4), lhsT_scale=g_s[:, n],
                    rhs=b_codes[:, m].bitcast(E4X4), rhs_scale=b_scales[:, m],
                    start=True, stop=True,
                )
            box["pr", c, g] = pp[:].rearrange("p t m -> p m t")

        def wave_tiles(c):
            if ("wv", c) not in box:
                wv = work.tile([P, 2, P, 4], F32, align_bytes=64, bufs=10, name="wv", tag="wv")
                turns = work.tile([P, 2, P, 4], I32, align_bytes=64, bufs=2, name="turns", tag="turns")
                box["wv", c] = wv
                box["tn", c] = turns

        def par_copy(c, g):
            wave_tiles(c)
            nc.scalar.activation(out=box["wv", c][:, g], in_=box["pr", c, g], func=ACT.Copy, bias=0.25, scale=1.0)

        def turns_gpsimd(c):
            nc.gpsimd.tensor_scalar(out=box["tn", c][:], in0=box["wv", c][:], scalar1=1.0, scalar2=0.0, op0=ALU.mult, op1=ALU.add)

        def turns_vector(c, g):
            wave_tiles(c)
            nc.vector.tensor_scalar(out=box["tn", c][:, g], in0=box["pr", c, g], scalar1=0.25, scalar2=None, op0=ALU.add)

        def rest(c, g):
            nc.vector.scalar_tensor_tensor(
                out=box["wv", c][:, g], in0=box["pr", c, g], scalar=0.25, in1=box["tn", c][:, g], op0=ALU.add, op1=ALU.subtract
            )

        def turns_sbuf(c):
            nc.vector.tensor_copy(out=box["tn", c][:], in_=box["wv", c][:])

        def rest_sbuf(c):
            nc.vector.tensor_tensor(out=box["wv", c][:], in0=box["wv", c][:], in1=box["tn", c][:], op=ALU.subtract)

        def wave(c):
            nc.scalar.activation(out=box["wv", c][:], in_=box["wv", c][:], func=ACT.Sin, scale=TWO_PI)

        amp_bc = amp_sb[:].rearrange("p (g t) -> p g t", g=2).unsqueeze(2).to_broadcast([P, 2, P, 4])

        def code_scale(c, half=None):
            if ("p4", c) not in box:
                cd = work.tile([P, 2, P, 4], BF16, align_bytes=64, bufs=8, name="cd", tag="cd")
                box["p4", c] = cd
            cd = box["p4", c]
            if half is None:
                nc.vector.tensor_tensor(out=cd[:], in0=box["wv", c][:], in1=amp_bc, op=ALU.mult)
            else:
                nc.gpsimd.tensor_tensor(out=cd[:, half], in0=box["wv", c][:, half], in1=amp_bc[:, half], op=ALU.mult)

        def code_quant(c):
            cq = work.tile([P, 2, P], U32, align_bytes=64, bufs=4, name="cq", tag="cq")
            cs = work.tile([P, 2, P], U8, align_bytes=64, bufs=4, name="cs", tag="cs")
            nc.vector.quantize_mx(
                out=cq[:].rearrange("p g m -> p (g m)").bitcast(E4X4), scales=cs[:].rearrange("p g m -> p (g m)"),
                in_=box["p4", c][:].rearrange("p g m t -> p (g m t)"),
            )
            box["qc", c] = (cq, cs)

        def product(c, rh):
            cq, cs = box["qc", c]
            po = psum.tile([P, 512], F32, bufs=3, tag="acc", name="po")
            r = slice(512 * rh, 512 * rh + 512)
            for h in range(2):
                nc.tensor.matmul_mx(
                    out=po[:],
                    lhsT=cq[:, h, :].bitcast(E4X4), lhsT_scale=cs[:, h, :],
                    rhs=y_codes[:, h, r].bitcast(E4X4), rhs_scale=y_scales[:, h, r],
                    start=(h == 0), stop=(h == 1),
                )
            box["mm", c, rh] = po

        def product_empty(c, rh):
            if rh == 0:
                res = work.tile([P, R], F32, align_bytes=64, bufs=3, name="res", tag="res")
                box["oc", c] = res
            dst = box["oc", c][:, 512 * rh : 512 * rh + 512]
            if not (c >= 10 and rh == 1):
                nc.scalar.copy(out=dst, in_=box["mm", c, rh][:])
            else:
                nc.vector.tensor_copy(out=dst, in_=box["mm", c, rh][:])

        def store(c):
            nc.sync.dma_start(out=out[P * c : P * c + P, :], in_=box["oc", c][:])

        steps = []

        def at(due, fn, *args):
            steps.append((due, len(steps), fn, args))

        at(0, permute_g)
        at(1, rx_widen, 0, 0)
        at(2, rx_widen, 0, 1)
        at(3, filt_turn, 0, 0)
        at(4, bits_turn, 0)
        at(5, bits_empty, 0)
        at(6, bits_quant, 0)
        at(7, filt_quant, 0, 0)
        at(8, rx_turn, 0, 0)
        at(9, rx_mult, 0, 0)
        at(10, filt_turn, 0, 1)
        at(11, par, 0, 0)
        at(12, rx_widen, 1, 0)
        at(13, par, 0, 1)
        at(14, rx_turn, 0, 1)
        at(15, turns_vector, 0, 0)
        at(16, filt_quant, 0, 1)
        at(17, rx_mult, 0, 1)
        at(18, turns_vector, 0, 1)
        at(19, rest, 0, 0)
        at(20, rest, 0, 1)
        at(21, filt_turn, 1, 0)
        at(22, bits_turn, 1)
        at(23, rx_turn, 0, 2)
        at(24, rx_quant, 0, 0)
        at(25, bits_empty, 1)
        at(26, par, 1, 0)
        at(27, par_copy, 1, 0)
        at(28, rx_mult, 0, 2)
        at(29, rx_widen, 1, 1)
        at(30, par, 1, 1)
        at(31, par_copy, 1, 1)
        at(32, bits_quant, 1)
        at(33, filt_quant, 1, 0)
        at(34, filt_turn, 1, 1)
        at(35, rx_turn, 1, 0)
        at(36, rx_quant, 0, 1)
        at(37, rx_mult, 1, 0)
        at(38, par, 2, 0)
        at(39, turns_gpsimd, 1)
        at(40, rest, 1, 0)
        at(41, par, 2, 1)
        at(42, rest, 1, 1)
        at(43, rx_widen, 2, 0)
        at(44, turns_vector, 2, 0)
        at(45, filt_turn, 2, 0)
        at(46, wave, 0)
        at(47, turns_vector, 2, 1)
        at(48, rx_turn, 1, 1)
        at(49, rx_mult, 1, 1)
        at(50, rest, 2, 0)
        at(51, filt_quant, 1, 1)
        at(52, rx_quant, 0, 2)
        at(53, rest, 2, 1)
        at(54, bits_turn, 2)
        at(55, bits_empty, 2)
        at(56, par, 3, 0)
        at(57, par_copy, 3, 0)
        at(58, rx_turn, 1, 2)
        at(59, rx_mult, 1, 2)
        at(60, par, 3, 1)
        at(61, par_copy, 3, 1)
        at(62, bits_quant, 2)
        at(63, wave, 1)
        at(64, filt_turn, 2, 1)
        at(65, rx_quant, 1, 0)
        at(66, rx_widen, 2, 1)
        at(67, filt_quant, 2, 0)
        at(68, rx_turn, 2, 0)
        at(69, rx_mult, 2, 0)
        at(70, wave, 2)
        at(71, turns_gpsimd, 3)
        at(72, rest, 3, 0)
        at(73, rest, 3, 1)
        at(74, rx_quant, 1, 1)
        at(75, par, 4, 0)
        at(76, par, 4, 1)
        at(77, turns_vector, 4, 0)
        at(78, bits_turn, 3)
        at(79, rx_widen, 3, 0)
        at(80, turns_vector, 4, 1)
        at(81, rest, 4, 0)
        at(82, bits_empty, 3)
        at(83, rest, 4, 1)
        at(84, filt_quant, 2, 1)
        at(85, rx_turn, 2, 1)
        at(86, rx_mult, 2, 1)
        at(87, wave, 3)
        at(88, rx_quant, 1, 2)
        at(89, turn_amp)
        at(90, sym, 0, 0)
        at(91, bits_quant, 3)
        at(92, par, 5, 0)
        at(93, par_copy, 5, 0)
        at(94, par, 5, 1)
        at(95, par_copy, 5, 1)
        at(96, rx_turn, 2, 2)
        at(97, rx_mult, 2, 2)
        at(98, sym, 0, 1)
        at(99, rx_widen, 3, 1)
        at(100, rx_quant, 2, 0)
        at(101, sym_empty, 0, 0)
        at(102, wave, 4)
        at(103, sym, 1, 0)
        at(104, turns_gpsimd, 5)
        at(105, rest, 5, 0)
        at(106, sym_empty, 0, 1)
        at(107, rx_turn, 3, 0)
        at(108, rx_mult, 3, 0)
        at(109, rest, 5, 1)
        at(110, bits_turn, 4)
        at(111, bits_empty, 4)
        at(112, sym, 1, 1)
        at(113, par, 6, 0)
        at(114, sym_empty, 1, 0)
        at(115, par, 6, 1)
        at(116, rx_quant, 2, 1)
        at(117, turns_vector, 6, 0)
        at(118, code_scale, 1, 0)
        at(119, code_scale, 1, 1)
        at(120, turns_vector, 6, 1)
        at(121, rest, 6, 0)
        at(122, sym_empty, 1, 1)
        at(123, sym, 2, 0)
        at(124, rest, 6, 1)
        at(125, wave, 5)
        at(126, rx_turn, 3, 1)
        at(127, rx_mult, 3, 1)
        at(128, sym_empty, 2, 0)
        at(129, bits_quant, 4)
        at(130, sym, 2, 1)
        at(131, rx_quant, 2, 2)
        at(132, sym_empty, 2, 1)
        at(133, code_scale, 2, 0)
        at(134, code_scale, 2, 1)
        at(135, par, 7, 0)
        at(136, par_copy, 7, 0)
        at(137, par, 7, 1)
        at(138, par_copy, 7, 1)
        at(139, sym, 3, 0)
        at(140, sym_empty, 3, 0)
        at(141, rx_turn, 3, 2)
        at(142, rx_mult, 3, 2)
        at(143, turns_gpsimd, 7)
        at(144, wave, 6)
        at(145, bits_turn, 5)
        at(146, bits_empty, 5)
        at(147, rx_quant, 3, 0)
        at(148, sym, 3, 1)
        at(149, sym_empty, 3, 1)
        at(150, code_scale, 3, 0)
        at(151, code_scale, 3, 1)
        at(152, rest, 7, 0)
        at(153, sym, 4, 0)
        at(154, sym_empty, 4, 0)
        at(155, par, 8, 0)
        at(156, rest, 7, 1)
        at(157, par, 8, 1)
        at(158, turns_vector, 8, 0)
        at(159, turns_vector, 8, 1)
        at(160, rx_quant, 3, 1)
        at(161, rest, 8, 0)
        at(162, wave, 7)
        at(163, sym, 4, 1)
        at(164, sym_empty, 4, 1)
        at(165, code_scale, 4, 0)
        at(166, sym_quant, 1, 0)
        at(167, rest, 8, 1)
        at(168, code_scale, 4, 1)
        at(169, bits_quant, 5)
        at(170, sym, 5, 0)
        at(171, sym_empty, 5, 0)
        at(172, par, 9, 0)
        at(173, par_copy, 9, 0)
        at(174, rx_quant, 3, 2)
        at(175, code_scale, 5, 0)
        at(176, bits_turn, 6)
        at(177, par, 9, 1)
        at(178, par_copy, 9, 1)
        at(179, turns_gpsimd, 9)
        at(180, bits_empty, 6)
        at(181, sym, 5, 1)
        at(182, sym_empty, 5, 1)
        at(183, code_scale, 5, 1)
        at(184, wave, 8)
        at(185, sym, 6, 0)
        at(186, sym_empty, 6, 0)
        at(187, code_scale, 6, 0)
        at(188, sym_quant, 0, 0)
        at(189, code_scale, 6, 1)
        at(190, sym, 6, 1)
        at(191, sym_empty, 6, 1)
        at(192, code_scale, 0)
        at(193, code_quant, 0)
        at(194, par, 10, 0)
        at(195, rest, 9, 0)
        at(196, code_quant, 1)
        at(197, par, 10, 1)
        at(198, rest, 9, 1)
        at(199, turns_vector, 10, 0)
        at(200, wave, 9)
        at(201, turns_vector, 10, 1)
        at(202, rest, 10, 0)
        at(203, bits_quant, 6)
        at(204, sym, 7, 0)
        at(205, sym_empty, 7, 0)
        at(206, rest, 10, 1)
        at(207, sym_quant, 0, 1)
        at(208, code_scale, 7, 0)
        at(209, code_quant, 2)
        at(210, code_scale, 7, 1)
        at(211, bits_turn, 7)
        at(212, sym, 7, 1)
        at(213, sym_empty, 7, 1)
        at(214, bits_empty, 7)
        at(215, sym_quant, 1, 1)
        at(216, par, 11, 0)
        at(217, code_quant, 3)
        at(218, par, 11, 1)
        at(219, turns_vector, 11, 0)
        at(220, wave, 10)
        at(221, code_scale, 8, 0)
        at(222, turns_vector, 11, 1)
        at(223, rest, 11, 0)
        at(224, code_scale, 8, 1)
        at(225, product, 0, 0)
        at(226, rest, 11, 1)
        at(227, product, 0, 1)
        at(228, product_empty, 0, 0)
        at(229, product_empty, 0, 1)
        at(230, code_quant, 4)
        at(231, product, 1, 0)
        at(232, product, 1, 1)
        at(233, product_empty, 1, 0)
        at(234, product_empty, 1, 1)
        at(235, par, 12, 0)
        at(236, code_scale, 9, 0)
        at(237, code_quant, 5)
        at(238, code_scale, 9, 1)
        at(239, store, 0)
        at(240, par, 12, 1)
        at(241, product, 2, 0)
        at(242, bits_quant, 7)
        at(243, wave, 11)
        at(244, product, 2, 1)
        at(245, turns_vector, 12, 0)
        at(246, product_empty, 2, 0)
        at(247, turns_vector, 12, 1)
        at(248, product_empty, 2, 1)
        at(249, rest, 12, 0)
        at(250, rest, 12, 1)
        at(251, store, 1)
        at(252, product, 3, 0)
        at(253, product, 3, 1)
        at(254, code_quant, 6)
        at(255, product_empty, 3, 0)
        at(256, product_empty, 3, 1)
        at(257, code_scale, 10, 0)
        at(258, code_scale, 10, 1)
        at(259, store, 2)
        at(260, product, 4, 0)
        at(261, product, 4, 1)
        at(262, par, 13, 0)
        at(263, product_empty, 4, 0)
        at(264, product_empty, 4, 1)
        at(265, code_quant, 7)
        at(266, par, 13, 1)
        at(267, wave, 12)
        at(268, turns_vector, 13, 0)
        at(269, store, 3)
        at(270, turns_vector, 13, 1)
        at(271, product, 5, 0)
        at(272, rest, 13, 0)
        at(273, product, 5, 1)
        at(274, rest, 13, 1)
        at(275, product_empty, 5, 0)
        at(276, code_scale, 11, 0)
        at(277, code_quant, 8)
        at(278, product_empty, 5, 1)
        at(279, code_scale, 11, 1)
        at(280, store, 4)
        at(281, product, 6, 0)
        at(282, product, 6, 1)
        at(283, product_empty, 6, 0)
        at(284, code_quant, 9)
        at(285, product_empty, 6, 1)
        at(286, store, 5)
        at(287, par, 14, 0)
        at(288, product, 7, 0)
        at(289, wave, 13)
        at(290, product, 7, 1)
        at(291, par, 14, 1)
        at(292, turns_vector, 14, 0)
        at(293, code_scale, 12, 0)
        at(294, product_empty, 7, 0)
        at(295, turns_vector, 14, 1)
        at(296, code_quant, 10)
        at(297, product_empty, 7, 1)
        at(298, rest, 14, 0)
        at(299, code_scale, 12, 1)
        at(300, store, 6)
        at(301, product, 8, 0)
        at(302, rest, 14, 1)
        at(303, product, 8, 1)
        at(304, product_empty, 8, 0)
        at(305, product_empty, 8, 1)
        at(306, code_quant, 11)
        at(307, product, 9, 0)
        at(308, store, 7)
        at(309, product, 9, 1)
        at(310, product_empty, 9, 0)
        at(311, product_empty, 9, 1)
        at(312, code_scale, 13, 0)
        at(313, par, 15, 0)
        at(314, wave, 14)
        at(315, store, 8)
        at(316, code_scale, 13, 1)
        at(317, product, 10, 0)
        at(318, product, 10, 1)
        at(319, code_quant, 12)
        at(320, par, 15, 1)
        at(321, turns_vector, 15, 0)
        at(322, product_empty, 10, 0)
        at(323, product_empty, 10, 1)
        at(324, turns_vector, 15, 1)
        at(325, store, 9)
        at(326, rest, 15, 0)
        at(327, product, 11, 0)
        at(328, rest, 15, 1)
        at(329, product, 11, 1)
        at(330, code_quant, 13)
        at(331, product_empty, 11, 0)
        at(332, store, 10)
        at(333, product_empty, 11, 1)
        at(334, code_scale, 14, 0)
        at(335, product, 12, 0)
        at(336, product, 12, 1)
        at(337, code_scale, 14, 1)
        at(338, store, 11)
        at(339, product_empty, 12, 0)
        at(340, product_empty, 12, 1)
        at(341, code_quant, 14)
        at(342, wave, 15)
        at(343, code_scale, 15)
        at(344, product, 13, 0)
        at(345, store, 12)
        at(346, product, 13, 1)
        at(347, product_empty, 13, 0)
        at(348, product_empty, 13, 1)
        at(349, code_quant, 15)
        at(350, store, 13)
        at(351, product, 14, 0)
        at(352, product, 14, 1)
        at(353, product_empty, 14, 0)
        at(354, product_empty, 14, 1)
        at(355, store, 14)
        at(356, product, 15, 0)
        at(357, product_empty, 15, 0)
        at(358, product, 15, 1)
        at(359, product_empty, 15, 1)
        at(360, store, 15)
        steps.sort(key=lambda s: s[:2])
        ctx.enter_context(tc.manual_schedule())
        for due, i, fn, args in steps:
            fn(*args)
